import numpy as np
import ml_dtypes


def mxq(x, axis, fmt="e4m3"):
    dtype, down = {"e4m3": (ml_dtypes.float8_e4m3fn, 7), "e5m2": (ml_dtypes.float8_e5m2, 14)}[fmt]
    v = np.moveaxis(np.asarray(x, np.float32).astype(ml_dtypes.bfloat16).astype(np.float64), axis, -1)
    blocks = v.reshape(v.shape[:-1] + (-1, 32))
    amax = np.abs(blocks).max(-1, keepdims=True)
    byte = np.maximum(np.where(amax > 0, np.frexp(amax)[1] - 1 + 127, 0) - down, 1)
    scale = np.exp2(byte - 127.0)
    codes = (blocks / scale).astype(np.float32).astype(dtype).astype(np.float64)
    return np.moveaxis((codes * scale).reshape(v.shape), -1, axis)


WIDE = False


def mx_kscale(k):
    if not WIDE:
        return np.ones(k)
    levels = np.array([10, -10, 5, -5, 0])
    if k % 512:
        return np.exp2(np.random.permutation(np.resize(levels, k // 32))).repeat(32)
    a = np.empty((k // 512, 16))
    for p in range(k // 512):
        a[p, :8] = np.random.permutation(np.resize(levels, 8))
        for g in range(8):
            far = levels[np.abs(levels - a[p, g]) >= 10]
            a[p, g + 8] = far[np.random.randint(len(far))]
    return np.exp2(a.ravel()).repeat(32)


def f64(x):
    return np.asarray(x).astype(np.float64)


def striped(idx):
    return np.tile(idx.reshape(-1, 16).T, (8, 1)).astype(np.uint16)


def unstriped(offs):
    return offs[:16].T.reshape(-1).astype(np.int64)


E2M1 = np.array([0.0, 0.5, 1.0, 1.5, 2.0, 3.0, 4.0, 6.0, -0.0, -0.5, -1.0, -1.5, -2.0, -3.0, -4.0, -6.0])


def pack_weight(w, fmt):
    k, n = w.shape
    w = f64(np.asarray(w, np.float32).astype(ml_dtypes.bfloat16)).reshape(k // 32, 32, n)
    amax = np.abs(w).max(1)
    if fmt == "e4m3":
        byte = np.frexp(amax)[1] - 1 + 127 - 7
    else:
        mant, ex = np.frexp(amax / 6.0)
        byte = np.where(mant > 0.5, ex, ex - 1) + 127
    byte = np.clip(np.where(amax > 0, byte, 1), 1, 254)
    scaled = (w * np.exp2(127.0 - byte)[:, None, :]).reshape(k, n).astype(np.float32)
    by_word = np.ascontiguousarray(scaled.reshape(k // 512, 128, 4, n).transpose(0, 1, 3, 2))
    if fmt == "e4m3":
        words = by_word.astype(ml_dtypes.float8_e4m3fn).view(np.uint8)
    else:
        c = by_word.astype(ml_dtypes.float4_e2m1fn).view(np.uint8) & 0xF
        words = (c[..., 0::2] | (c[..., 1::2] << 4)).reshape(k // 512, 128, 2 * n)
    return np.ascontiguousarray(words), np.ascontiguousarray(byte.astype(np.uint8).reshape(k // 512, 16, n))


def unpack_weight(words, scales, fmt):
    g, _, n = scales.shape
    words = np.ascontiguousarray(words).reshape(g, 128, n, -1)
    if fmt == "e4m3":
        vals = words.view(ml_dtypes.float8_e4m3fn).astype(np.float64)
    else:
        nib = np.empty((g, 128, n, 4), np.uint8)
        nib[..., 0::2] = words & 0xF
        nib[..., 1::2] = words >> 4
        vals = E2M1[nib]
    vals = vals * np.repeat(np.exp2(scales.astype(np.float64) - 127.0), 8, axis=1)[..., None]
    return vals.transpose(0, 1, 3, 2).reshape(g * 512, n)


def gelu(v):
    return 0.5 * v * (1.0 + np.tanh(np.sqrt(2.0 / np.pi) * (v + 0.044715 * v**3)))


K, T, S, H, T2, P, N = 512, 2048, 1024, 1024, 2048, 1024, 512


def setup_inputs():
    n = np.random.standard_normal
    s = mx_kscale(K)[:, None]
    u = mx_kscale(H)[:, None]
    tab_words, tab_scales = pack_weight(n((K, T)) * s, "e4m3")
    w2_words, w2_scales = pack_weight(1.2 * n((H, N)) / np.sqrt(H) / u, "e2m1")
    return {
        "tab_words": tab_words,
        "tab_scales": tab_scales,
        "offs": striped(np.random.permutation(T)[:S]),
        "w1": (1.7 * n((K, H)) / np.sqrt(K) / s).astype(np.float32),
        "b1": (0.7 * n(H)).astype(np.float32),
        "gain": (np.random.uniform(1.2, 2.2, H) * u[:, 0]).astype(np.float32),
        "page0": (n((H, T2)) * u).astype(np.float32),
        "offs2": striped(np.random.permutation(T2)[:S]),
        "offs3": striped(np.random.permutation(T2)[:P]),
        "w2_words": w2_words,
        "w2_scales": w2_scales,
        "w3": (1.3 * n((K, N)) / np.sqrt(K) / s).astype(np.float32),
        "b2": (0.6 * n(N)).astype(np.float32),
    }


def reference(tab_words, tab_scales, offs, w1, b1, gain, page0, offs2, offs3, w2_words, w2_scales, w3, b2):
    v = unpack_weight(tab_words, tab_scales, "e4m3")[:, unstriped(offs)]
    w2 = unpack_weight(w2_words, w2_scales, "e2m1")
    d = mxq(f64(w1), 0, "e4m3").T @ v
    h = f64(gain)[:, None] * np.tanh(d + f64(b1)[:, None])
    page = f64(page0).copy()
    l2 = unstriped(offs2)
    page[:, l2] = page[:, l2] + h
    x = page[:, unstriped(offs3)]
    y = w2.T @ mxq(x, 0, "e4m3") + mxq(f64(w3), 0, "e4m3").T @ v
    return 1.0 / (1.0 + np.exp(-(y + f64(b2)[:, None])))

@@ -1,0 +1,232 @@
+from contextlib import ExitStack
+
+import concourse.mybir as mybir
+
+K, T, S, H, T2, N = 512, 2048, 1024, 1024, 2048, 512
+FLOPS = 2 * S * (K * H + H * N + K * N)
+
+F32 = mybir.dt.float32
+BF16 = mybir.dt.bfloat16
+I32 = mybir.dt.int32
+U32 = mybir.dt.uint32
+U16 = mybir.dt.uint16
+U8 = mybir.dt.uint8
+E4M3X4 = mybir.dt.float8_e4m3fn_x4
+E2M1X4 = mybir.dt.float4_e2m1fn_x4
+ACT = mybir.ActivationFunctionType
+ADD = mybir.AluOpType.add
+
+P = 128
+PACK = 4
+K_PASS = P * PACK
+H_PASSES = H // K_PASS
+SLICES = H_PASSES * PACK
+N_TILES = N // P
+BANK = 512
+CHUNKS = (256, 256, 256, 256)
+
+
+def tile_list_street_leak_callout_kernel(
+    tc, tab_words, tab_scales, offs, w1, b1, gain, page0, offs2, offs3, w2_words, w2_scales, w3, b2, out
+):
+    nc = tc.nc
+    with ExitStack() as ctx:
+        keep = ctx.enter_context(tc.tile_pool(name="keep", bufs=1))
+        ring = ctx.enter_context(tc.tile_pool(name="ring", bufs=2))
+        psum = ctx.enter_context(tc.psum_pool(name="psum", bufs=1))
+
+        def bank(i):
+            return psum.tile([P, BANK], F32, name=f"bank{i}", tag=f"bank{i}")
+
+        def load_scale_rows(tile, rows):
+            for q in range(4):
+                nc.scalar.dma_start(out=tile[32 * q : 32 * q + 4, :].bitcast(I32), in_=rows(q).bitcast(I32))
+
+        list1 = keep.tile([P, S // 16], U16)
+        list2 = keep.tile([P, S // 16], U16)
+        list3 = keep.tile([P, S // 16], U16)
+        table_words = keep.tile([P, T], I32)
+        table_scales = keep.tile([P, T], U8)
+        w2_codes = keep.tile([P, H_PASSES, 2 * N], U8, align_bytes=64)
+        w2_plane = keep.tile([P, H_PASSES, N], U8, align_bytes=64)
+        b1_sb = keep.tile([P, H_PASSES, PACK], F32)
+        gain_sb = keep.tile([P, H_PASSES, PACK], F32)
+        b2_sb = keep.tile([P, N_TILES], F32)
+        pages = [keep.tile([P, T2], F32, name=f"page{s}") for s in range(SLICES)]
+        w1_raw = [keep.tile([P, PACK, K_PASS], F32, name=f"w1_raw{a}") for a in range(H_PASSES)]
+        w3_raw = keep.tile([P, PACK, N], F32)
+        page_rows = page0.rearrange("(a p t) c -> a t p c", a=H_PASSES, t=PACK)
+        w1_rows = w1.rearrange("(p j) r -> p j r", j=PACK)
+
+        def load_page(s):
+            nc.sync.dma_start(out=pages[s][:], in_=page_rows[s // PACK, s % PACK])
+
+        def load_w1(a):
+            nc.sync.dma_start(out=w1_raw[a][:], in_=w1_rows[:, :, a * K_PASS : (a + 1) * K_PASS])
+
+        nc.vector.memset(table_scales[:].bitcast(I32), 0)
+        nc.vector.memset(w2_plane[:].rearrange("p a n -> p (a n)").bitcast(I32), 0)
+
+        nc.sync.dma_start(list1[:], offs)
+        nc.sync.dma_start(out=table_words[:], in_=tab_words[0].rearrange("p t i -> p (t i)").bitcast(I32))
+        load_scale_rows(table_scales, lambda q: tab_scales[0, 4 * q : 4 * q + 4, :])
+        load_w1(0)
+        nc.sync.dma_start(list2[:], offs2)
+        load_page(0)
+        nc.sync.dma_start(out=b1_sb[:], in_=b1.rearrange("(a p t) -> p a t", a=H_PASSES, t=PACK))
+        nc.sync.dma_start(out=gain_sb[:], in_=gain.rearrange("(a p t) -> p a t", a=H_PASSES, t=PACK))
+        load_page(1)
+        load_page(2)
+        load_w1(1)
+        load_page(3)
+        nc.sync.dma_start(out=w3_raw[:], in_=w3.rearrange("(p j) n -> p j n", j=PACK))
+        for s in range(4, SLICES):
+            load_page(s)
+        nc.sync.dma_start(list3[:], offs3)
+        nc.sync.dma_start(out=w2_codes[:].bitcast(I32), in_=w2_words.rearrange("a p c -> p a c").bitcast(I32))
+        for q in range(4):
+            nc.sync.dma_start(
+                out=w2_plane[32 * q : 32 * q + 4, :, :].bitcast(I32),
+                in_=w2_scales[:, 4 * q : 4 * q + 4, :].rearrange("a r n -> r a n").bitcast(I32),
+            )
+        with nc.allow_non_contiguous_dma(reason="one bias value per partition and output tile"):
+            nc.sync.dma_start(out=b2_sb[:], in_=b2.rearrange("(t p) -> p t", p=P))
+
+        v_words = keep.tile([P, S], U32, align_bytes=64)
+        v_plane = keep.tile([P, S], U8, align_bytes=64)
+        nc.vector.tensor_copy(out=v_words[:], in_=table_words[:].bitcast(U32).indirect(list1[:]))
+        nc.vector.tensor_copy(out=v_plane[:], in_=table_scales[:].indirect(list1[:]))
+
+        w1_codes = keep.tile([P, H], U32, align_bytes=64)
+        w1_planes = [keep.tile([P, K_PASS], U8, name=f"w1_plane{a}", align_bytes=64) for a in range(H_PASSES)]
+        w3_codes = keep.tile([P, N], U32, align_bytes=64)
+        w3_plane = keep.tile([P, N], U8, align_bytes=64)
+
+        def weave_w1(a):
+            woven = keep.tile([P, K_PASS * PACK], BF16, name=f"w1_woven{a}", align_bytes=64)
+            nc.scalar.copy(
+                out=woven[:].rearrange("p (t m j) -> p m j t", t=PACK, j=PACK),
+                in_=w1_raw[a][:].rearrange("p j (m t) -> p m j t", t=PACK),
+            )
+            return woven
+
+        def quantize_w1(a, woven):
+            nc.vector.quantize_mx(
+                out=w1_codes[:, a * K_PASS : (a + 1) * K_PASS].bitcast(E4M3X4), scales=w1_planes[a][:], in_=woven[:]
+            )
+
+        def fetch_old(s):
+            old = keep.tile([P, S], F32, name=f"old{s}", tag=f"old{s % 2}", align_bytes=64)
+            nc.vector.tensor_copy(out=old[:], in_=pages[s][:].indirect(list2[:]))
+            return old
+
+        def make_h(s):
+            a, t = divmod(s, PACK)
+            h = keep.tile([P, S], F32, name=f"h{s}", tag=f"h{s % 2}", align_bytes=64)
+            for half in range(S // BANK):
+                cols = slice(half * BANK, (half + 1) * BANK)
+                d = bank(2 * (s % 2) + half)
+                nc.tensor.matmul_mx(
+                    out=d[:],
+                    lhsT=w1_codes[:, s * P : (s + 1) * P].bitcast(E4M3X4),
+                    lhsT_scale=w1_planes[a][:, t * P : (t + 1) * P],
+                    rhs=v_words[:, cols].bitcast(E4M3X4),
+                    rhs_scale=v_plane[:, cols],
+                    start=True,
+                    stop=True,
+                )
+                bounded = ring.tile([P, BANK], F32)
+                nc.scalar.activation(out=bounded[:], in_=d[:], func=ACT.Tanh, bias=b1_sb[:, a, t : t + 1])
+                nc.scalar.activation(out=h[:, cols], in_=bounded[:], func=ACT.Copy, scale=gain_sb[:, a, t : t + 1])
+            return h
+
+        def put_new(s, old, h):
+            nc.vector.tensor_tensor(out=pages[s][:].indirect(list2[:]), in0=old[:], in1=h[:], op=ADD)
+
+        woven0 = weave_w1(0)
+        quantize_w1(0, woven0)
+        old = fetch_old(0)
+        for s in range(SLICES):
+            h = make_h(s)
+            next_old = fetch_old(s + 1) if s + 1 < SLICES else None
+            put_new(s, old, h)
+            old = next_old
+            if s == 0:
+                quantize_w1(1, weave_w1(1))
+            if s == 2:
+                w3_woven = keep.tile([P, N * PACK], BF16, align_bytes=64)
+                nc.scalar.copy(
+                    out=w3_woven[:].rearrange("p (c i j) -> p c j i", i=4, j=PACK),
+                    in_=w3_raw[:].rearrange("p j (c i) -> p c j i", i=4),
+                )
+                nc.vector.quantize_mx(out=w3_codes[:].bitcast(E4M3X4), scales=w3_plane[:], in_=w3_woven[:])
+
+        last = (SLICES - 1) % 2
+        slots = (f"old{last}", f"h{last}")
+        out_rows = out.rearrange("(t p) j -> p t j", p=P)
+        starts = [sum(CHUNKS[:c]) for c in range(len(CHUNKS))]
+        groups = [(c, a) for c in range(len(CHUNKS)) for a in range(H_PASSES)]
+
+        def fetch_x(c, a):
+            j0, width = starts[c], CHUNKS[c]
+            picked = keep.tile([P, PACK, width], BF16, name=f"picked{c}_{a}", tag=slots[a], align_bytes=64)
+            for t in range(PACK):
+                nc.vector.tensor_copy(
+                    out=picked[:, t, :], in_=pages[a * PACK + t][:].indirect(list3[:, j0 // 16 : (j0 + width) // 16])
+                )
+            woven = ring.tile([P, width * PACK], BF16, name=f"x_woven{c}_{a}", tag="x_woven", align_bytes=64)
+            nc.scalar.copy(
+                out=woven[:].rearrange("p (c i t) -> p c t i", i=4, t=PACK),
+                in_=picked[:].rearrange("p t (c i) -> p c t i", i=4),
+            )
+            return woven
+
+        sums = {}
+
+        def score(c, a, woven):
+            j0, width = starts[c], CHUNKS[c]
+            cols = slice(j0, j0 + width)
+            x_codes = ring.tile([P, width], U32, name=f"x_codes{c}_{a}", tag="x_codes", align_bytes=64)
+            x_plane = ring.tile([P, width], U8, name=f"x_plane{c}_{a}", tag="x_plane", align_bytes=64)
+            nc.vector.quantize_mx(out=x_codes[:].bitcast(E4M3X4), scales=x_plane[:], in_=woven[:])
+            if a == 0:
+                sums[c] = [bank(N_TILES * ((c + 1) % 2) + n) for n in range(N_TILES)]
+                for n in range(N_TILES):
+                    nc.tensor.matmul_mx(
+                        out=sums[c][n][:, :width],
+                        lhsT=w3_codes[:, n * P : (n + 1) * P].bitcast(E4M3X4),
+                        lhsT_scale=w3_plane[:, n * P : (n + 1) * P],
+                        rhs=v_words[:, cols].bitcast(E4M3X4),
+                        rhs_scale=v_plane[:, cols],
+                        start=True,
+                        stop=False,
+                    )
+            closing = a == H_PASSES - 1
+            if closing:
+                scores = ring.tile([P, N_TILES, width], F32, name=f"scores{c}", tag="scores")
+            for n in range(N_TILES):
+                nc.tensor.matmul_mx(
+                    out=sums[c][n][:, :width],
+                    lhsT=w2_codes[:, a, 2 * n * P : 2 * (n + 1) * P].bitcast(E2M1X4),
+                    lhsT_scale=w2_plane[:, a, n * P : (n + 1) * P],
+                    rhs=x_codes[:].bitcast(E4M3X4),
+                    rhs_scale=x_plane[:],
+                    start=False,
+                    stop=closing,
+                )
+                if closing:
+                    nc.scalar.activation(
+                        out=scores[:, n, :], in_=sums[c][n][:, :width], func=ACT.Sigmoid, bias=b2_sb[:, n : n + 1]
+                    )
+                    if c == len(CHUNKS) - 1:
+                        nc.sync.dma_start(out=out_rows[:, n, cols], in_=scores[:, n, :])
+            if closing and c < len(CHUNKS) - 1:
+                nc.sync.dma_start(out=out_rows[:, :, cols], in_=scores[:])
+
+        waiting = None
+        for c, a in groups:
+            woven = fetch_x(c, a)
+            if waiting is not None:
+                score(*waiting)
+            waiting = (c, a, woven)
+        score(*waiting)

@@ -23,7 +23,8 @@ H_PASSES = H // K_PASS
 SLICES = H_PASSES * PACK
 N_TILES = N // P
 BANK = 512
-CHUNKS = (256, 256, 256, 256)
+AHEAD = 2
+CHUNKS = (256, 256, 256, 128, 128)
 
 
 def tile_list_street_leak_callout_kernel(
@@ -40,7 +41,7 @@ def tile_list_street_leak_callout_kernel(
 
         def load_scale_rows(tile, rows):
             for q in range(4):
-                nc.scalar.dma_start(out=tile[32 * q : 32 * q + 4, :].bitcast(I32), in_=rows(q).bitcast(I32))
+                nc.sync.dma_start(out=tile[32 * q : 32 * q + 4, :].bitcast(I32), in_=rows(q).bitcast(I32))
 
         list1 = keep.tile([P, S // 16], U16)
         list2 = keep.tile([P, S // 16], U16)
@@ -50,16 +51,21 @@ def tile_list_street_leak_callout_kernel(
         w2_codes = keep.tile([P, H_PASSES, 2 * N], U8, align_bytes=64)
         w2_plane = keep.tile([P, H_PASSES, N], U8, align_bytes=64)
         b1_sb = keep.tile([P, H_PASSES, PACK], F32)
-        gain_sb = keep.tile([P, H_PASSES, PACK], F32)
+        gains = [keep.tile([P, 1], F32, name=f"gain{s}") for s in range(SLICES)]
         b2_sb = keep.tile([P, N_TILES], F32)
         pages = [keep.tile([P, T2], F32, name=f"page{s}") for s in range(SLICES)]
         w1_raw = [keep.tile([P, PACK, K_PASS], F32, name=f"w1_raw{a}") for a in range(H_PASSES)]
         w3_raw = keep.tile([P, PACK, N], F32)
         page_rows = page0.rearrange("(a p t) c -> a t p c", a=H_PASSES, t=PACK)
+        gain_rows = gain.rearrange("(a p t) -> a p t", a=H_PASSES, t=PACK)
         w1_rows = w1.rearrange("(p j) r -> p j r", j=PACK)
 
         def load_page(s):
             nc.sync.dma_start(out=pages[s][:], in_=page_rows[s // PACK, s % PACK])
+
+        def load_gain(s):
+            with nc.allow_non_contiguous_dma(reason="one gain value per partition"):
+                nc.sync.dma_start(out=gains[s][:], in_=gain_rows[s // PACK, :, s % PACK : s % PACK + 1])
 
         def load_w1(a):
             nc.sync.dma_start(out=w1_raw[a][:], in_=w1_rows[:, :, a * K_PASS : (a + 1) * K_PASS])
@@ -70,18 +76,19 @@ def tile_list_street_leak_callout_kernel(
         nc.sync.dma_start(list1[:], offs)
         nc.sync.dma_start(out=table_words[:], in_=tab_words[0].rearrange("p t i -> p (t i)").bitcast(I32))
         load_scale_rows(table_scales, lambda q: tab_scales[0, 4 * q : 4 * q + 4, :])
-        load_w1(0)
         nc.sync.dma_start(list2[:], offs2)
         load_page(0)
+        load_w1(0)
         nc.sync.dma_start(out=b1_sb[:], in_=b1.rearrange("(a p t) -> p a t", a=H_PASSES, t=PACK))
-        nc.sync.dma_start(out=gain_sb[:], in_=gain.rearrange("(a p t) -> p a t", a=H_PASSES, t=PACK))
-        load_page(1)
-        load_page(2)
-        load_w1(1)
-        load_page(3)
-        nc.sync.dma_start(out=w3_raw[:], in_=w3.rearrange("(p j) n -> p j n", j=PACK))
-        for s in range(4, SLICES):
-            load_page(s)
+        for s in range(1, SLICES + AHEAD):
+            if s < SLICES:
+                load_page(s)
+            if s >= AHEAD:
+                load_gain(s - AHEAD)
+            if s == 3:
+                load_w1(1)
+            if s == 5:
+                nc.sync.dma_start(out=w3_raw[:], in_=w3.rearrange("(p j) n -> p j n", j=PACK))
         nc.sync.dma_start(list3[:], offs3)
         nc.sync.dma_start(out=w2_codes[:].bitcast(I32), in_=w2_words.rearrange("a p c -> p a c").bitcast(I32))
         for q in range(4):
@@ -102,21 +109,20 @@ def tile_list_street_leak_callout_kernel(
         w3_codes = keep.tile([P, N], U32, align_bytes=64)
         w3_plane = keep.tile([P, N], U8, align_bytes=64)
 
-        def weave_w1(a):
-            woven = keep.tile([P, K_PASS * PACK], BF16, name=f"w1_woven{a}", align_bytes=64)
+        def quantize_w1(a, t0, t1):
+            woven = ring.tile([P, (t1 - t0) * P * PACK], BF16, name=f"w1_woven{a}_{t0}", tag="w1_woven", align_bytes=64)
             nc.scalar.copy(
-                out=woven[:].rearrange("p (t m j) -> p m j t", t=PACK, j=PACK),
-                in_=w1_raw[a][:].rearrange("p j (m t) -> p m j t", t=PACK),
+                out=woven[:].rearrange("p (t m j) -> p m j t", m=P, j=PACK),
+                in_=w1_raw[a][:].rearrange("p j (m t) -> p m j t", t=PACK)[:, :, :, t0:t1],
             )
-            return woven
-
-        def quantize_w1(a, woven):
             nc.vector.quantize_mx(
-                out=w1_codes[:, a * K_PASS : (a + 1) * K_PASS].bitcast(E4M3X4), scales=w1_planes[a][:], in_=woven[:]
+                out=w1_codes[:, a * K_PASS + t0 * P : a * K_PASS + t1 * P].bitcast(E4M3X4),
+                scales=w1_planes[a][:, t0 * P : t1 * P],
+                in_=woven[:],
             )
 
         def fetch_old(s):
-            old = keep.tile([P, S], F32, name=f"old{s}", tag=f"old{s % 2}", align_bytes=64)
+            old = keep.tile([P, S], F32, name=f"old{s}", tag=f"old{s % (AHEAD + 2)}", align_bytes=64)
             nc.vector.tensor_copy(out=old[:], in_=pages[s][:].indirect(list2[:]))
             return old
 
@@ -137,22 +143,23 @@ def tile_list_street_leak_callout_kernel(
                 )
                 bounded = ring.tile([P, BANK], F32)
                 nc.scalar.activation(out=bounded[:], in_=d[:], func=ACT.Tanh, bias=b1_sb[:, a, t : t + 1])
-                nc.scalar.activation(out=h[:, cols], in_=bounded[:], func=ACT.Copy, scale=gain_sb[:, a, t : t + 1])
+                nc.scalar.activation(out=h[:, cols], in_=bounded[:], func=ACT.Copy, scale=gains[s][:])
             return h
 
         def put_new(s, old, h):
             nc.vector.tensor_tensor(out=pages[s][:].indirect(list2[:]), in0=old[:], in1=h[:], op=ADD)
 
-        woven0 = weave_w1(0)
-        quantize_w1(0, woven0)
-        old = fetch_old(0)
+        olds = [fetch_old(0)]
+        quantize_w1(0, 0, PACK // 2)
+        quantize_w1(0, PACK // 2, PACK)
+        olds.extend(fetch_old(s) for s in range(1, AHEAD))
         for s in range(SLICES):
             h = make_h(s)
-            next_old = fetch_old(s + 1) if s + 1 < SLICES else None
-            put_new(s, old, h)
-            old = next_old
+            if s + AHEAD < SLICES:
+                olds.append(fetch_old(s + AHEAD))
+            put_new(s, olds[s], h)
             if s == 0:
-                quantize_w1(1, weave_w1(1))
+                quantize_w1(1, 0, PACK)
             if s == 2:
                 w3_woven = keep.tile([P, N * PACK], BF16, align_bytes=64)
                 nc.scalar.copy(
@@ -161,8 +168,7 @@ def tile_list_street_leak_callout_kernel(
                 )
                 nc.vector.quantize_mx(out=w3_codes[:].bitcast(E4M3X4), scales=w3_plane[:], in_=w3_woven[:])
 
-        last = (SLICES - 1) % 2
-        slots = (f"old{last}", f"h{last}")
+        slots = (f"h{(SLICES - 2) % 2}", f"h{(SLICES - 1) % 2}")
         out_rows = out.rearrange("(t p) j -> p t j", p=P)
         starts = [sum(CHUNKS[:c]) for c in range(len(CHUNKS))]
         groups = [(c, a) for c in range(len(CHUNKS)) for a in range(H_PASSES)]
@@ -175,7 +181,8 @@ def tile_list_street_leak_callout_kernel(
                     out=picked[:, t, :], in_=pages[a * PACK + t][:].indirect(list3[:, j0 // 16 : (j0 + width) // 16])
                 )
             woven = ring.tile([P, width * PACK], BF16, name=f"x_woven{c}_{a}", tag="x_woven", align_bytes=64)
-            nc.scalar.copy(
+            weave = nc.vector.tensor_copy if (c, a) == groups[-1] else nc.scalar.copy
+            weave(
                 out=woven[:].rearrange("p (c i t) -> p c t i", i=4, t=PACK),
                 in_=picked[:].rearrange("p t (c i) -> p c t i", i=4),
             )

from contextlib import ExitStack

import concourse.mybir as mybir

K, T, S, H, T2, N = 512, 2048, 1024, 1024, 2048, 512
FLOPS = 2 * S * (K * H + H * N + K * N)

F32 = mybir.dt.float32
BF16 = mybir.dt.bfloat16
I32 = mybir.dt.int32
U32 = mybir.dt.uint32
U16 = mybir.dt.uint16
U8 = mybir.dt.uint8
E4M3X4 = mybir.dt.float8_e4m3fn_x4
E2M1X4 = mybir.dt.float4_e2m1fn_x4
ACT = mybir.ActivationFunctionType
ADD = mybir.AluOpType.add

P = 128
PACK = 4
K_PASS = P * PACK
H_PASSES = H // K_PASS
SLICES = H_PASSES * PACK
N_TILES = N // P
BANK = 512
AHEAD = 2
CHUNKS = (256, 256, 256, 128, 128)


def tile_list_street_leak_callout_kernel(
    tc, tab_words, tab_scales, offs, w1, b1, gain, page0, offs2, offs3, w2_words, w2_scales, w3, b2, out
):
    nc = tc.nc
    with ExitStack() as ctx:
        keep = ctx.enter_context(tc.tile_pool(name="keep", bufs=1))
        ring = ctx.enter_context(tc.tile_pool(name="ring", bufs=2))
        psum = ctx.enter_context(tc.psum_pool(name="psum", bufs=1))

        def bank(i):
            return psum.tile([P, BANK], F32, name=f"bank{i}", tag=f"bank{i}")

        def load_scale_rows(tile, rows):
            for q in range(4):
                nc.sync.dma_start(out=tile[32 * q : 32 * q + 4, :].bitcast(I32), in_=rows(q).bitcast(I32))

        list1 = keep.tile([P, S // 16], U16)
        list2 = keep.tile([P, S // 16], U16)
        list3 = keep.tile([P, S // 16], U16)
        table_words = keep.tile([P, T], I32)
        table_scales = keep.tile([P, T], U8)
        w2_codes = keep.tile([P, H_PASSES, 2 * N], U8, align_bytes=64)
        w2_plane = keep.tile([P, H_PASSES, N], U8, align_bytes=64)
        b1_sb = keep.tile([P, H_PASSES, PACK], F32)
        gains = [keep.tile([P, 1], F32, name=f"gain{s}") for s in range(SLICES)]
        b2_sb = keep.tile([P, N_TILES], F32)
        pages = [keep.tile([P, T2], F32, name=f"page{s}") for s in range(SLICES)]
        w1_raw = [keep.tile([P, PACK, K_PASS], F32, name=f"w1_raw{a}") for a in range(H_PASSES)]
        w3_raw = keep.tile([P, PACK, N], F32)
        page_rows = page0.rearrange("(a p t) c -> a t p c", a=H_PASSES, t=PACK)
        gain_rows = gain.rearrange("(a p t) -> a p t", a=H_PASSES, t=PACK)
        w1_rows = w1.rearrange("(p j) r -> p j r", j=PACK)

        def load_page(s):
            nc.sync.dma_start(out=pages[s][:], in_=page_rows[s // PACK, s % PACK])

        def load_gain(s):
            with nc.allow_non_contiguous_dma(reason="one gain value per partition"):
                nc.sync.dma_start(out=gains[s][:], in_=gain_rows[s // PACK, :, s % PACK : s % PACK + 1])

        def load_w1(a):
            nc.sync.dma_start(out=w1_raw[a][:], in_=w1_rows[:, :, a * K_PASS : (a + 1) * K_PASS])

        nc.vector.memset(table_scales[:].bitcast(I32), 0)
        nc.vector.memset(w2_plane[:].rearrange("p a n -> p (a n)").bitcast(I32), 0)

        nc.sync.dma_start(list1[:], offs)
        nc.sync.dma_start(out=table_words[:], in_=tab_words[0].rearrange("p t i -> p (t i)").bitcast(I32))
        load_scale_rows(table_scales, lambda q: tab_scales[0, 4 * q : 4 * q + 4, :])
        nc.sync.dma_start(list2[:], offs2)
        load_page(0)
        load_w1(0)
        nc.sync.dma_start(out=b1_sb[:], in_=b1.rearrange("(a p t) -> p a t", a=H_PASSES, t=PACK))
        for s in range(1, SLICES + AHEAD):
            if s < SLICES:
                load_page(s)
            if s >= AHEAD:
                load_gain(s - AHEAD)
            if s == 3:
                load_w1(1)
            if s == 5:
                nc.sync.dma_start(out=w3_raw[:], in_=w3.rearrange("(p j) n -> p j n", j=PACK))
        nc.sync.dma_start(list3[:], offs3)
        nc.sync.dma_start(out=w2_codes[:].bitcast(I32), in_=w2_words.rearrange("a p c -> p a c").bitcast(I32))
        for q in range(4):
            nc.sync.dma_start(
                out=w2_plane[32 * q : 32 * q + 4, :, :].bitcast(I32),
                in_=w2_scales[:, 4 * q : 4 * q + 4, :].rearrange("a r n -> r a n").bitcast(I32),
            )
        with nc.allow_non_contiguous_dma(reason="one bias value per partition and output tile"):
            nc.sync.dma_start(out=b2_sb[:], in_=b2.rearrange("(t p) -> p t", p=P))

        v_words = keep.tile([P, S], U32, align_bytes=64)
        v_plane = keep.tile([P, S], U8, align_bytes=64)
        nc.vector.tensor_copy(out=v_words[:], in_=table_words[:].bitcast(U32).indirect(list1[:]))
        nc.vector.tensor_copy(out=v_plane[:], in_=table_scales[:].indirect(list1[:]))

        w1_codes = keep.tile([P, H], U32, align_bytes=64)
        w1_planes = [keep.tile([P, K_PASS], U8, name=f"w1_plane{a}", align_bytes=64) for a in range(H_PASSES)]
        w3_codes = keep.tile([P, N], U32, align_bytes=64)
        w3_plane = keep.tile([P, N], U8, align_bytes=64)

        def quantize_w1(a, t0, t1):
            woven = ring.tile([P, (t1 - t0) * P * PACK], BF16, name=f"w1_woven{a}_{t0}", tag="w1_woven", align_bytes=64)
            nc.scalar.copy(
                out=woven[:].rearrange("p (t m j) -> p m j t", m=P, j=PACK),
                in_=w1_raw[a][:].rearrange("p j (m t) -> p m j t", t=PACK)[:, :, :, t0:t1],
            )
            nc.vector.quantize_mx(
                out=w1_codes[:, a * K_PASS + t0 * P : a * K_PASS + t1 * P].bitcast(E4M3X4),
                scales=w1_planes[a][:, t0 * P : t1 * P],
                in_=woven[:],
            )

        def fetch_old(s):
            old = keep.tile([P, S], F32, name=f"old{s}", tag=f"old{s % (AHEAD + 2)}", align_bytes=64)
            nc.vector.tensor_copy(out=old[:], in_=pages[s][:].indirect(list2[:]))
            return old

        def make_h(s):
            a, t = divmod(s, PACK)
            h = keep.tile([P, S], F32, name=f"h{s}", tag=f"h{s % 2}", align_bytes=64)
            for half in range(S // BANK):
                cols = slice(half * BANK, (half + 1) * BANK)
                d = bank(2 * (s % 2) + half)
                nc.tensor.matmul_mx(
                    out=d[:],
                    lhsT=w1_codes[:, s * P : (s + 1) * P].bitcast(E4M3X4),
                    lhsT_scale=w1_planes[a][:, t * P : (t + 1) * P],
                    rhs=v_words[:, cols].bitcast(E4M3X4),
                    rhs_scale=v_plane[:, cols],
                    start=True,
                    stop=True,
                )
                bounded = ring.tile([P, BANK], F32)
                nc.scalar.activation(out=bounded[:], in_=d[:], func=ACT.Tanh, bias=b1_sb[:, a, t : t + 1])
                nc.scalar.activation(out=h[:, cols], in_=bounded[:], func=ACT.Copy, scale=gains[s][:])
            return h

        def put_new(s, old, h):
            nc.vector.tensor_tensor(out=pages[s][:].indirect(list2[:]), in0=old[:], in1=h[:], op=ADD)

        olds = [fetch_old(0)]
        quantize_w1(0, 0, PACK // 2)
        quantize_w1(0, PACK // 2, PACK)
        olds.extend(fetch_old(s) for s in range(1, AHEAD))
        for s in range(SLICES):
            h = make_h(s)
            if s + AHEAD < SLICES:
                olds.append(fetch_old(s + AHEAD))
            put_new(s, olds[s], h)
            if s == 0:
                quantize_w1(1, 0, PACK)
            if s == 2:
                w3_woven = keep.tile([P, N * PACK], BF16, align_bytes=64)
                nc.scalar.copy(
                    out=w3_woven[:].rearrange("p (c i j) -> p c j i", i=4, j=PACK),
                    in_=w3_raw[:].rearrange("p j (c i) -> p c j i", i=4),
                )
                nc.vector.quantize_mx(out=w3_codes[:].bitcast(E4M3X4), scales=w3_plane[:], in_=w3_woven[:])

        slots = (f"h{(SLICES - 2) % 2}", f"h{(SLICES - 1) % 2}")
        out_rows = out.rearrange("(t p) j -> p t j", p=P)
        starts = [sum(CHUNKS[:c]) for c in range(len(CHUNKS))]
        groups = [(c, a) for c in range(len(CHUNKS)) for a in range(H_PASSES)]

        def fetch_x(c, a):
            j0, width = starts[c], CHUNKS[c]
            picked = keep.tile([P, PACK, width], BF16, name=f"picked{c}_{a}", tag=slots[a], align_bytes=64)
            for t in range(PACK):
                nc.vector.tensor_copy(
                    out=picked[:, t, :], in_=pages[a * PACK + t][:].indirect(list3[:, j0 // 16 : (j0 + width) // 16])
                )
            woven = ring.tile([P, width * PACK], BF16, name=f"x_woven{c}_{a}", tag="x_woven", align_bytes=64)
            weave = nc.vector.tensor_copy if (c, a) == groups[-1] else nc.scalar.copy
            weave(
                out=woven[:].rearrange("p (c i t) -> p c t i", i=4, t=PACK),
                in_=picked[:].rearrange("p t (c i) -> p c t i", i=4),
            )
            return woven

        sums = {}

        def score(c, a, woven):
            j0, width = starts[c], CHUNKS[c]
            cols = slice(j0, j0 + width)
            x_codes = ring.tile([P, width], U32, name=f"x_codes{c}_{a}", tag="x_codes", align_bytes=64)
            x_plane = ring.tile([P, width], U8, name=f"x_plane{c}_{a}", tag="x_plane", align_bytes=64)
            nc.vector.quantize_mx(out=x_codes[:].bitcast(E4M3X4), scales=x_plane[:], in_=woven[:])
            if a == 0:
                sums[c] = [bank(N_TILES * ((c + 1) % 2) + n) for n in range(N_TILES)]
                for n in range(N_TILES):
                    nc.tensor.matmul_mx(
                        out=sums[c][n][:, :width],
                        lhsT=w3_codes[:, n * P : (n + 1) * P].bitcast(E4M3X4),
                        lhsT_scale=w3_plane[:, n * P : (n + 1) * P],
                        rhs=v_words[:, cols].bitcast(E4M3X4),
                        rhs_scale=v_plane[:, cols],
                        start=True,
                        stop=False,
                    )
            closing = a == H_PASSES - 1
            if closing:
                scores = ring.tile([P, N_TILES, width], F32, name=f"scores{c}", tag="scores")
            for n in range(N_TILES):
                nc.tensor.matmul_mx(
                    out=sums[c][n][:, :width],
                    lhsT=w2_codes[:, a, 2 * n * P : 2 * (n + 1) * P].bitcast(E2M1X4),
                    lhsT_scale=w2_plane[:, a, n * P : (n + 1) * P],
                    rhs=x_codes[:].bitcast(E4M3X4),
                    rhs_scale=x_plane[:],
                    start=False,
                    stop=closing,
                )
                if closing:
                    nc.scalar.activation(
                        out=scores[:, n, :], in_=sums[c][n][:, :width], func=ACT.Sigmoid, bias=b2_sb[:, n : n + 1]
                    )
                    if c == len(CHUNKS) - 1:
                        nc.sync.dma_start(out=out_rows[:, n, cols], in_=scores[:, n, :])
            if closing and c < len(CHUNKS) - 1:
                nc.sync.dma_start(out=out_rows[:, :, cols], in_=scores[:])

        waiting = None
        for c, a in groups:
            woven = fetch_x(c, a)
            if waiting is not None:
                score(*waiting)
            waiting = (c, a, woven)
        score(*waiting)
